import numpy as np
import ml_dtypes


def mxq(x, axis, fmt="e4m3"):
    dtype, down = {"e4m3": (ml_dtypes.float8_e4m3fn, 7), "e5m2": (ml_dtypes.float8_e5m2, 14)}[fmt]
    v = np.moveaxis(np.asarray(x, np.float32).astype(ml_dtypes.bfloat16).astype(np.float64), axis, -1)
    blocks = v.reshape(v.shape[:-1] + (-1, 32))
    amax = np.abs(blocks).max(-1, keepdims=True)
    byte = np.maximum(np.where(amax > 0, np.frexp(amax)[1] - 1 + 127, 0) - down, 1)
    scale = np.exp2(byte - 127.0)
    codes = (blocks / scale).astype(np.float32).astype(dtype).astype(np.float64)
    return np.moveaxis((codes * scale).reshape(v.shape), -1, axis)


WIDE = False


def mx_kscale(k):
    if not WIDE:
        return np.ones(k)
    levels = np.array([10, -10, 5, -5, 0])
    if k % 512:
        return np.exp2(np.random.permutation(np.resize(levels, k // 32))).repeat(32)
    a = np.empty((k // 512, 16))
    for p in range(k // 512):
        a[p, :8] = np.random.permutation(np.resize(levels, 8))
        for g in range(8):
            far = levels[np.abs(levels - a[p, g]) >= 10]
            a[p, g + 8] = far[np.random.randint(len(far))]
    return np.exp2(a.ravel()).repeat(32)


def f64(x):
    return np.asarray(x).astype(np.float64)


def striped(idx):
    return np.tile(np.asarray(idx).reshape(-1, 16).T, (8, 1)).astype(np.uint16)


def unstriped(offs):
    return offs[:16].T.reshape(-1).astype(np.int64)


def striped8(idx):
    return np.asarray(idx).reshape(8, -1, 16).transpose(0, 2, 1).reshape(128, -1).astype(np.uint16)


def unstriped8(offs):
    return offs.reshape(8, 16, -1).transpose(0, 2, 1).reshape(8, -1).astype(np.int64)


def pick8(x, idx, run):
    r = np.arange(len(x))
    return x[r[:, None], idx[r % (8 * run) // run]]


E2M1 = np.array([0.0, 0.5, 1.0, 1.5, 2.0, 3.0, 4.0, 6.0, -0.0, -0.5, -1.0, -1.5, -2.0, -3.0, -4.0, -6.0])


def pack_weight(w, fmt):
    k, n = w.shape
    w = f64(np.asarray(w, np.float32).astype(ml_dtypes.bfloat16)).reshape(k // 32, 32, n)
    amax = np.abs(w).max(1)
    if fmt == "e4m3":
        byte = np.frexp(amax)[1] - 1 + 127 - 7
    else:
        mant, ex = np.frexp(amax / 6.0)
        byte = np.where(mant > 0.5, ex, ex - 1) + 127
    byte = np.clip(np.where(amax > 0, byte, 1), 1, 254)
    scaled = (w * np.exp2(127.0 - byte)[:, None, :]).reshape(k, n).astype(np.float32)
    by_word = np.ascontiguousarray(scaled.reshape(k // 512, 128, 4, n).transpose(0, 1, 3, 2))
    if fmt == "e4m3":
        words = by_word.astype(ml_dtypes.float8_e4m3fn).view(np.uint8)
    else:
        c = by_word.astype(ml_dtypes.float4_e2m1fn).view(np.uint8) & 0xF
        words = (c[..., 0::2] | (c[..., 1::2] << 4)).reshape(k // 512, 128, 2 * n)
    return np.ascontiguousarray(words), np.ascontiguousarray(byte.astype(np.uint8).reshape(k // 512, 16, n))


def unpack_weight(words, scales, fmt):
    g, _, n = scales.shape
    words = np.ascontiguousarray(words).reshape(g, 128, n, -1)
    if fmt == "e4m3":
        vals = words.view(ml_dtypes.float8_e4m3fn).astype(np.float64)
    else:
        nib = np.empty((g, 128, n, 4), np.uint8)
        nib[..., 0::2] = words & 0xF
        nib[..., 1::2] = words >> 4
        vals = E2M1[nib]
    vals = vals * np.repeat(np.exp2(scales.astype(np.float64) - 127.0), 8, axis=1)[..., None]
    return vals.transpose(0, 1, 3, 2).reshape(g * 512, n)


def sigmoid(v):
    return 1.0 / (1.0 + np.exp(-v))


K, R, F, T, J, M, G = 512, 128, 512, 2048, 512, 256, 32


def setup_inputs():
    n = np.random.standard_normal
    idx = np.random.permutation(T)[:J]
    idx2 = np.stack([np.random.permutation(J)[:M] for _ in range(8)])
    fk = mx_kscale(K)
    ff = mx_kscale(F)
    tabp = pack_weight(n((K, T)) / fk[:, None], "e4m3")
    dtabp = pack_weight(n((K, T)) / fk[:, None], "e4m3")
    return {
        "tab_words": tabp[0],
        "tab_scales": tabp[1],
        "w1": (n((K, R)) * 1 / np.sqrt(K) * fk[:, None]).astype(np.float32),
        "gain": (np.random.uniform(0.5, 1.5, (R, 1))).astype(np.float32),
        "pb": (np.random.uniform(-0.7, 0.7, (1, M))).astype(np.float32),
        "wo": (n((F, R)) * 1 / np.sqrt(F) * ff[:, None]).astype(np.float32),
        "dy": (n((F, M)) / ff[:, None]).astype(np.float32),
        "dtab_words": dtabp[0],
        "dtab_scales": dtabp[1],
        "og": (np.random.uniform(0.7, 2.0, (R, 1))).astype(np.float32),
        "base": (0.3 * n((R, J))).astype(np.float32),
        "offs": striped(idx),
        "offs2": striped8(idx2),
    }


def reference(tab_words, tab_scales, w1, gain, pb, wo, dy, dtab_words, dtab_scales, og, base, offs, offs2):
    idx = unstriped(offs)
    idx2 = unstriped8(offs2)
    tabu = unpack_weight(tab_words, tab_scales, "e4m3")
    dtabu = unpack_weight(dtab_words, dtab_scales, "e4m3")
    w1q = mxq(f64(w1), 0, "e4m3")
    tabidxg = tabu[:, idx]
    a = w1q.T @ tabidxg
    dtabidxg = dtabu[:, idx]
    ta = w1q.T @ dtabidxg
    h1 = a * f64(gain)
    s = pick8(h1, idx2, 16) + f64(pb)
    q2 = np.sqrt(np.square(s).reshape(R, G, M // G).mean(axis=2) + 0.1)
    qr = np.repeat(q2, M // G, axis=1)
    woq = mxq(f64(wo), 0, "e4m3")
    dyq = mxq(f64(dy), 0, "e4m3")
    c0 = woq.T @ dyq
    dqr = c0 * sigmoid(s / qr) * (1.0 + s / qr * (1.0 - sigmoid(s / qr))) * s / np.square(qr) * (-1.0)
    dq2 = dqr.reshape(R, G, M // G).sum(axis=2)
    e1 = dq2 * 0.5 / np.sqrt(np.square(s).reshape(R, G, M // G).mean(axis=2) + 0.1) / 8.0
    r1 = np.repeat(e1, M // G, axis=1)
    xh1 = ta * f64(gain)
    xs = pick8(xh1, idx2, 16)
    xq2 = (xs * s * 2.0).reshape(R, G, M // G).mean(axis=2) * 0.5 / q2
    xqr = np.repeat(xq2, M // G, axis=1)
    xdqr = (((xs - xqr * s / qr) / qr * sigmoid(s / qr) * (1.0 - sigmoid(s / qr)) * (1.0 + s / qr * (1.0 - sigmoid(s / qr))) + ((xs - xqr * s / qr) / qr * (1.0 - sigmoid(s / qr)) + (xs - xqr * s / qr) / qr * sigmoid(s / qr) * (1.0 - sigmoid(s / qr)) * (-1.0) * s / qr) * sigmoid(s / qr)) * c0 * s + xs * c0 * sigmoid(s / qr) * (1.0 + s / qr * (1.0 - sigmoid(s / qr))) - xqr * qr * 2.0 * c0 * sigmoid(s / qr) * (1.0 + s / qr * (1.0 - sigmoid(s / qr))) * s / np.square(qr)) / np.square(qr) * (-1.0)
    xdq2 = xdqr.reshape(R, G, M // G).sum(axis=2)
    xe1 = (xdq2 * 0.5 - (xs * s * 2.0).reshape(R, G, M // G).mean(axis=2) * 0.5 / np.sqrt(np.square(s).reshape(R, G, M // G).mean(axis=2) + 0.1) * dq2 * 0.5 / np.sqrt(np.square(s).reshape(R, G, M // G).mean(axis=2) + 0.1)) / np.sqrt(np.square(s).reshape(R, G, M // G).mean(axis=2) + 0.1) / 8.0
    xr1 = np.repeat(xe1, M // G, axis=1)
    xds = (((xs - xqr * s / qr) / qr * sigmoid(s / qr) * (1.0 - sigmoid(s / qr)) * (1.0 + s / qr * (1.0 - sigmoid(s / qr))) + ((xs - xqr * s / qr) / qr * (1.0 - sigmoid(s / qr)) + (xs - xqr * s / qr) / qr * sigmoid(s / qr) * (1.0 - sigmoid(s / qr)) * (-1.0) * s / qr) * sigmoid(s / qr)) * c0 - xqr * c0 * sigmoid(s / qr) * (1.0 + s / qr * (1.0 - sigmoid(s / qr))) / qr) / qr + (xr1 * s + xs * r1) * 2.0
    xs2 = np.zeros((R, J))
    xs2[np.arange(R)[:, None], idx2[np.arange(R) % 128 // 16]] = xds
    xda = xs2 * f64(gain)
    y = xda * f64(og) + f64(base)
    return y

@@ -1,0 +1,213 @@
+from contextlib import ExitStack
+
+import concourse.mybir as mybir
+from concourse.masks import make_identity
+
+F32 = mybir.dt.float32
+BF16 = mybir.dt.bfloat16
+I32 = mybir.dt.int32
+U32 = mybir.dt.uint32
+U16 = mybir.dt.uint16
+U8 = mybir.dt.uint8
+FP8X4 = mybir.dt.float8_e4m3fn_x4
+ACT = mybir.ActivationFunctionType
+ALU = mybir.AluOpType
+AX = mybir.AxisListType
+
+P = 128
+PACK = 4
+K, R, F, T, J, M, G = 512, 128, 512, 2048, 512, 256, 32
+GS = M // G
+
+FLOPS = 2 * K * R * J * 2 + 2 * F * R * M
+
+
+def tile_attend_hvcpickscaled_kernel(tc, tab_words, tab_scales, w1, gain, pb, wo, dy, dtab_words, dtab_scales,
+                                      og, base, offs, offs2, out):
+    nc = tc.nc
+    add, mult, sub = ALU.add, ALU.mult, ALU.subtract
+
+    with ExitStack() as ctx:
+        lists = ctx.enter_context(tc.tile_pool(name="lists", bufs=1))
+        keep = ctx.enter_context(tc.tile_pool(name="keep", bufs=1))
+        psum = ctx.enter_context(tc.psum_pool(name="psum", bufs=1))
+
+        def sb(name, width, dtype=F32, tag=None):
+            return keep.tile([P, width], dtype, name=name, tag=tag or name, align_bytes=64)
+
+        def grouped(ap):
+            return ap.rearrange("p (g j) -> p g j", j=GS)
+
+        def spread(ap):
+            return ap.unsqueeze(2).to_broadcast([P, G, GS])
+
+        offs_sb = lists.tile([P, J // 16], U16, name="offs_sb")
+        offs2_sb = lists.tile([P, M // 16], U16, name="offs2_sb")
+
+        tab_w = sb("tab_w", T, U32)
+        tab_s, dtab_s = sb("tab_s", T, U8, tag="slot_wo"), sb("dtab_s", T, U8)
+        w1_raw = sb("w1_raw", PACK * R, tag="slot_dtab")
+        gain_sb, og_sb, pb_col = sb("gain_sb", 1), sb("og_sb", 1), sb("pb_col", 2)
+        placed = sb("placed", J)
+        ident = sb("ident", P, tag="slot_dy")
+
+        def load_words(tile, words):
+            nc.sync.dma_start(out=tile[:].bitcast(I32), in_=words[0].rearrange("p n t -> p (n t)").bitcast(I32))
+
+        def load_scales(queue, tile, scales, quads):
+            for quad in quads:
+                queue.dma_start(out=tile[32 * quad:32 * quad + 4, :].bitcast(I32),
+                                in_=scales[0, 4 * quad:4 * quad + 4, :].bitcast(I32))
+
+        def load_rows(tile, rows):
+            nc.sync.dma_start(out=tile[:], in_=rows.rearrange("(p t) w -> p (t w)", t=PACK))
+
+        nc.vector.memset(tab_s[:].bitcast(I32), 0)
+        nc.vector.memset(dtab_s[:].bitcast(I32), 0)
+        warm = sb("warm", 1)
+        nc.vector.memset(warm[:], 1.0)
+        nc.vector.memset(placed[:], 0.0)
+
+        nc.sync.dma_start(offs_sb[:], offs)
+        nc.sync.dma_start(offs2_sb[:], offs2)
+        load_words(tab_w, tab_words)
+        load_rows(w1_raw, w1)
+        load_scales(nc.scalar, tab_s, tab_scales, range(4))
+        load_scales(nc.scalar, dtab_s, dtab_scales, range(2))
+        make_identity(nc, ident[:])
+        nc.gpsimd.dma_start(out=pb_col[:], in_=pb.rearrange("o (p h) -> (o p) h", h=2))
+        nc.gpsimd.dma_start(out=gain_sb[:], in_=gain)
+        load_scales(nc.gpsimd, dtab_s, dtab_scales, range(2, 4))
+        nc.gpsimd.dma_start(out=og_sb[:], in_=og)
+        warm2 = sb("warm2", 1)
+        nc.scalar.activation(warm2[:], warm[:], ACT.Sqrt)
+
+        def interleave(name, raw, width):
+            woven = sb(name + "_bf", PACK * width, BF16)
+            nc.scalar.copy(out=woven[:].rearrange("p (c i t) -> p c t i", t=PACK, i=4),
+                           in_=raw[:].rearrange("p (t c i) -> p c t i", t=PACK, i=4))
+            return woven
+
+        def quantise(name, woven, width):
+            codes, scales = sb(name + "_c", width, U32), sb(name + "_s", width, U8)
+            nc.vector.quantize_mx(out=codes[:].bitcast(FP8X4), scales=scales[:], in_=woven[:])
+            return codes, scales
+
+        def gather_tab(name, window, dtype):
+            picked = sb(name, J, dtype)
+            nc.vector.tensor_copy(picked[:], window[:].indirect(offs_sb[:]))
+            return picked
+
+        def product(name, lhs, rhs, width):
+            acc = psum.tile([P, width], F32, name=name)
+            nc.tensor.matmul_mx(out=acc[:], lhsT=lhs[0][:].bitcast(FP8X4), lhsT_scale=lhs[1][:],
+                                rhs=rhs[0][:].bitcast(FP8X4), rhs_scale=rhs[1][:], start=True, stop=True)
+            return acc
+
+        def tt(name, a, b, op):
+            res = sb(name, M)
+            nc.vector.tensor_tensor(res[:], a, b, op)
+            return res
+
+        def stt(name, a, scalar, b, op0, op1, width=M):
+            res = sb(name, width)
+            nc.vector.scalar_tensor_tensor(res[:], a, scalar, b, op0, op1)
+            return res
+
+        def stt_spread(name, small, scalar, b, op0, op1):
+            res = sb(name, M)
+            nc.vector.scalar_tensor_tensor(grouped(res[:]), spread(small), scalar, grouped(b), op0, op1)
+            return res
+
+        def act(name, a, func, width=M, **kw):
+            res = sb(name, width)
+            nc.scalar.activation(res[:], a, func, **kw)
+            return res
+
+        def group_sums(name, a, count=1):
+            res = sb(name, count * G)
+            nc.vector.tensor_reduce(res[:], grouped(a), AX.X, add)
+            return res
+
+        pb_ps = psum.tile([P, 2, P], F32, name="pb_ps")
+        for h in range(2):
+            nc.tensor.transpose(pb_ps[:, h, :], pb_col[:, h:h + 1].to_broadcast([P, P]), ident[:])
+        pb_full = sb("pb_full", M)
+        nc.scalar.copy(out=pb_full[:].rearrange("p (n h) -> p n h", h=2), in_=pb_ps[:].rearrange("p h n -> p n h"))
+        row_scale = sb("row_scale", 1)
+        nc.gpsimd.tensor_scalar(row_scale[:], gain_sb[:], og_sb[:], 0.5, mult, mult)
+
+        tab_gs = gather_tab("tab_gs", tab_s, U8)
+        wo_raw = sb("wo_raw", PACK * R, tag="slot_wo")
+        load_rows(wo_raw, wo)
+        dy_raw = sb("dy_raw", PACK * M, tag="slot_dy")
+        load_rows(dy_raw, dy)
+        tab_gw = gather_tab("tab_gw", tab_w, U32)
+        w1_bf = interleave("w1", w1_raw, R)
+        dtab_w = sb("dtab_w", T, U32, tag="slot_dtab")
+        load_words(dtab_w, dtab_words)
+        w1_q = quantise("w1", w1_bf, R)
+        a_ps = product("a_ps", w1_q, (tab_gw, tab_gs), J)
+        wo_bf = interleave("wo", wo_raw, R)
+        base_sb = sb("base_sb", J, tag="slot_wo")
+        nc.sync.dma_start(out=base_sb[:], in_=base)
+        h1 = act("h1", a_ps[:], ACT.Copy, width=J, scale=gain_sb[:])
+        dtab_gs = gather_tab("dtab_gs", dtab_s, U8)
+        dy_bf = interleave("dy", dy_raw, M)
+
+        s = sb("s", M)
+        nc.vector.tensor_tensor(s[:], h1[:].indirect(offs2_sb[:]), pb_full[:], add)
+        wo_q = quantise("wo", wo_bf, R)
+        s_sq = tt("s_sq", s[:], s[:], mult)
+        sq_sum = group_sums("sq_sum", s_sq[:])
+        q = act("q", sq_sum[:], ACT.Sqrt, width=G, scale=1.0 / GS, bias=0.1)
+        dtab_gw = gather_tab("dtab_gw", dtab_w, U32)
+        ta_ps = product("ta_ps", w1_q, (dtab_gw, dtab_gs), J)
+        rq = sb("rq", G)
+        nc.vector.reciprocal(rq[:], q[:])
+        dy_q = quantise("dy", dy_bf, M)
+        c_ps = product("c_ps", wo_q, dy_q, M)
+        u = sb("u", M)
+        nc.vector.tensor_tensor(grouped(u[:]), grouped(s[:]), spread(rq[:]), mult)
+
+        silu_neg = act("silu_neg", u[:], ACT.Silu, scale=-1.0)
+        th = act("th", u[:], ACT.Tanh, scale=-0.5)
+        xh1 = act("xh1", ta_ps[:], ACT.Copy, width=J, scale=gain_sb[:])
+        rq2 = sb("rq2", M)
+        nc.scalar.activation(grouped(rq2[:]), spread(rq[:]), ACT.Square)
+
+        bend = stt("bend", u[:], 0.5, silu_neg[:], mult, add)
+        c_sig = stt("c_sig", th[:], -1.0, c_ps[:], add, mult)
+        c_bell = stt("c_bell", th[:], 1.0, c_sig[:], add, mult)
+        f = stt("f", silu_neg[:], -1.0, c_sig[:], add, mult)
+        g = stt("g", bend[:], -1.0, c_bell[:], add, mult)
+        prods = sb("prods", 2 * M)
+        nc.vector.tensor_tensor(prods[:, 0:M], f[:], u[:], mult)
+        gu = tt("gu", g[:], u[:], mult)
+        x = sb("x", M)
+        nc.vector.tensor_tensor(x[:], xh1[:].indirect(offs2_sb[:]), rq2[:], mult)
+        e = tt("e", gu[:], f[:], add)
+        xprods = sb("xprods", 2 * M)
+        nc.vector.tensor_tensor(xprods[:, 0:M], x[:], u[:], mult)
+        nc.vector.tensor_tensor(prods[:, M:2 * M], e[:], u[:], mult)
+        nc.vector.tensor_tensor(xprods[:, M:2 * M], x[:], e[:], mult)
+        ab = group_sums("ab", prods[:], 2)
+        pq = group_sums("pq", xprods[:], 2)
+        sum_a, sum_b, sum_p, sum_q = ab[:, 0:G], ab[:, G:2 * G], pq[:, 0:G], pq[:, G:2 * G]
+        d = stt("d", sum_a, 2.0, sum_b, mult, add, width=G)
+        k = stt_spread("k", sum_a, -1.0 / GS, g[:], mult, add)
+        pd = stt("pd", sum_p, 1.0 / GS, d[:], mult, mult, width=G)
+        pe = stt_spread("pe", sum_p, -1.0 / GS, e[:], mult, mult)
+        z = sb("z", G)
+        nc.vector.tensor_tensor(z[:], pd[:], sum_q, sub)
+        xk = tt("xk", x[:], k[:], mult)
+        uz = stt_spread("uz", z[:], 1.0 / GS, u[:], mult, mult)
+        part = tt("part", xk[:], pe[:], add)
+        nc.vector.tensor_tensor(placed[:].indirect(offs2_sb[:]), part[:], uz[:], add)
+
+        res = sb("res", J)
+        half = J // 2
+        for i, queue in enumerate((nc.sync, nc.scalar)):
+            cols = slice(i * half, (i + 1) * half)
+            nc.vector.scalar_tensor_tensor(res[:, cols], placed[:, cols], row_scale[:], base_sb[:, cols], mult, add)
+            queue.dma_start(out=out[:, cols], in_=res[:, cols])

@@ -1,3 +1,4 @@
+import math
 from contextlib import ExitStack
 
 import concourse.mybir as mybir
@@ -44,12 +45,13 @@ def tile_attend_hvcpickscaled_kernel(tc, tab_words, tab_scales, w1, gain, pb, wo
         offs_sb = lists.tile([P, J // 16], U16, name="offs_sb")
         offs2_sb = lists.tile([P, M // 16], U16, name="offs2_sb")
 
-        tab_w = sb("tab_w", T, U32)
-        tab_s, dtab_s = sb("tab_s", T, U8, tag="slot_wo"), sb("dtab_s", T, U8)
-        w1_raw = sb("w1_raw", PACK * R, tag="slot_dtab")
+        tab_w, dtab_w = sb("tab_w", T, U32), sb("dtab_w", T, U32)
+        tab_s = sb("tab_s", T, U8)
+        w1_raw, wo_raw, dy_raw = sb("w1_raw", PACK * R, tag="w1_slot"), sb("wo_raw", PACK * R), sb("dy_raw", PACK * M)
         gain_sb, og_sb, pb_col = sb("gain_sb", 1), sb("og_sb", 1), sb("pb_col", 2)
+        base_sb = sb("base_sb", J)
         placed = sb("placed", J)
-        ident = sb("ident", P, tag="slot_dy")
+        ident = sb("ident", P)
 
         def load_words(tile, words):
             nc.sync.dma_start(out=tile[:].bitcast(I32), in_=words[0].rearrange("p n t -> p (n t)").bitcast(I32))
@@ -62,25 +64,26 @@ def tile_attend_hvcpickscaled_kernel(tc, tab_words, tab_scales, w1, gain, pb, wo
         def load_rows(tile, rows):
             nc.sync.dma_start(out=tile[:], in_=rows.rearrange("(p t) w -> p (t w)", t=PACK))
 
-        nc.vector.memset(tab_s[:].bitcast(I32), 0)
-        nc.vector.memset(dtab_s[:].bitcast(I32), 0)
         warm = sb("warm", 1)
         nc.vector.memset(warm[:], 1.0)
+        nc.vector.memset(tab_s[:].bitcast(I32), 0)
         nc.vector.memset(placed[:], 0.0)
-
-        nc.sync.dma_start(offs_sb[:], offs)
-        nc.sync.dma_start(offs2_sb[:], offs2)
-        load_words(tab_w, tab_words)
-        load_rows(w1_raw, w1)
-        load_scales(nc.scalar, tab_s, tab_scales, range(4))
-        load_scales(nc.scalar, dtab_s, dtab_scales, range(2))
-        make_identity(nc, ident[:])
-        nc.gpsimd.dma_start(out=pb_col[:], in_=pb.rearrange("o (p h) -> (o p) h", h=2))
-        nc.gpsimd.dma_start(out=gain_sb[:], in_=gain)
-        load_scales(nc.gpsimd, dtab_s, dtab_scales, range(2, 4))
-        nc.gpsimd.dma_start(out=og_sb[:], in_=og)
         warm2 = sb("warm2", 1)
         nc.scalar.activation(warm2[:], warm[:], ACT.Sqrt)
+
+        nc.sync.dma_start(offs_sb[:], offs)
+        nc.sync.dma_start(out=pb_col[:], in_=pb.rearrange("o (p h) -> (o p) h", h=2))
+        load_rows(w1_raw, w1)
+        load_scales(nc.sync, tab_s, tab_scales, range(4))
+        load_words(tab_w, tab_words)
+        nc.sync.dma_start(out=gain_sb[:], in_=gain)
+        nc.sync.dma_start(offs2_sb[:], offs2)
+        load_rows(dy_raw, dy)
+        load_rows(wo_raw, wo)
+        load_words(dtab_w, dtab_words)
+        nc.sync.dma_start(out=base_sb[:], in_=base)
+        nc.sync.dma_start(out=og_sb[:], in_=og)
+        make_identity(nc, ident[:])
 
         def interleave(name, raw, width):
             woven = sb(name + "_bf", PACK * width, BF16)
@@ -129,52 +132,46 @@ def tile_attend_hvcpickscaled_kernel(tc, tab_words, tab_scales, w1, gain, pb, wo
             nc.vector.tensor_reduce(res[:], grouped(a), AX.X, add)
             return res
 
+        w1_bf = interleave("w1", w1_raw, R)
         pb_ps = psum.tile([P, 2, P], F32, name="pb_ps")
         for h in range(2):
             nc.tensor.transpose(pb_ps[:, h, :], pb_col[:, h:h + 1].to_broadcast([P, P]), ident[:])
         pb_full = sb("pb_full", M)
         nc.scalar.copy(out=pb_full[:].rearrange("p (n h) -> p n h", h=2), in_=pb_ps[:].rearrange("p h n -> p n h"))
-        row_scale = sb("row_scale", 1)
-        nc.gpsimd.tensor_scalar(row_scale[:], gain_sb[:], og_sb[:], 0.5, mult, mult)
+        dtab_s = sb("dtab_s", T, U8, tag="w1_slot")
+        nc.vector.memset(dtab_s[:].bitcast(I32), 0)
+        load_scales(nc.scalar, dtab_s, dtab_scales, range(4))
 
         tab_gs = gather_tab("tab_gs", tab_s, U8)
-        wo_raw = sb("wo_raw", PACK * R, tag="slot_wo")
-        load_rows(wo_raw, wo)
-        dy_raw = sb("dy_raw", PACK * M, tag="slot_dy")
-        load_rows(dy_raw, dy)
-        tab_gw = gather_tab("tab_gw", tab_w, U32)
-        w1_bf = interleave("w1", w1_raw, R)
-        dtab_w = sb("dtab_w", T, U32, tag="slot_dtab")
-        load_words(dtab_w, dtab_words)
         w1_q = quantise("w1", w1_bf, R)
+        tab_gw = gather_tab("tab_gw", tab_w, U32)
         a_ps = product("a_ps", w1_q, (tab_gw, tab_gs), J)
-        wo_bf = interleave("wo", wo_raw, R)
-        base_sb = sb("base_sb", J, tag="slot_wo")
-        nc.sync.dma_start(out=base_sb[:], in_=base)
         h1 = act("h1", a_ps[:], ACT.Copy, width=J, scale=gain_sb[:])
         dtab_gs = gather_tab("dtab_gs", dtab_s, U8)
         dy_bf = interleave("dy", dy_raw, M)
+        wo_bf = interleave("wo", wo_raw, R)
 
         s = sb("s", M)
         nc.vector.tensor_tensor(s[:], h1[:].indirect(offs2_sb[:]), pb_full[:], add)
-        wo_q = quantise("wo", wo_bf, R)
         s_sq = tt("s_sq", s[:], s[:], mult)
         sq_sum = group_sums("sq_sum", s_sq[:])
         q = act("q", sq_sum[:], ACT.Sqrt, width=G, scale=1.0 / GS, bias=0.1)
-        dtab_gw = gather_tab("dtab_gw", dtab_w, U32)
-        ta_ps = product("ta_ps", w1_q, (dtab_gw, dtab_gs), J)
+        dy_q = quantise("dy", dy_bf, M)
         rq = sb("rq", G)
         nc.vector.reciprocal(rq[:], q[:])
-        dy_q = quantise("dy", dy_bf, M)
+        wo_q = quantise("wo", wo_bf, R)
         c_ps = product("c_ps", wo_q, dy_q, M)
         u = sb("u", M)
         nc.vector.tensor_tensor(grouped(u[:]), grouped(s[:]), spread(rq[:]), mult)
+        dtab_gw = gather_tab("dtab_gw", dtab_w, U32)
+        ta_ps = product("ta_ps", w1_q, (dtab_gw, dtab_gs), J)
 
         silu_neg = act("silu_neg", u[:], ACT.Silu, scale=-1.0)
         th = act("th", u[:], ACT.Tanh, scale=-0.5)
+        rq2 = sb("rq2", M, tag="s")
+        nc.scalar.activation(grouped(rq2[:]), spread(rq[:]), ACT.Square, scale=math.sqrt(0.5))
         xh1 = act("xh1", ta_ps[:], ACT.Copy, width=J, scale=gain_sb[:])
-        rq2 = sb("rq2", M)
-        nc.scalar.activation(grouped(rq2[:]), spread(rq[:]), ACT.Square)
+        row_scale = act("row_scale", og_sb[:], ACT.Copy, width=1, scale=gain_sb[:])
 
         bend = stt("bend", u[:], 0.5, silu_neg[:], mult, add)
         c_sig = stt("c_sig", th[:], -1.0, c_ps[:], add, mult)

import math
from contextlib import ExitStack

import concourse.mybir as mybir
from concourse.masks import make_identity

F32 = mybir.dt.float32
BF16 = mybir.dt.bfloat16
I32 = mybir.dt.int32
U32 = mybir.dt.uint32
U16 = mybir.dt.uint16
U8 = mybir.dt.uint8
FP8X4 = mybir.dt.float8_e4m3fn_x4
ACT = mybir.ActivationFunctionType
ALU = mybir.AluOpType
AX = mybir.AxisListType

P = 128
PACK = 4
K, R, F, T, J, M, G = 512, 128, 512, 2048, 512, 256, 32
GS = M // G

FLOPS = 2 * K * R * J * 2 + 2 * F * R * M


def tile_attend_hvcpickscaled_kernel(tc, tab_words, tab_scales, w1, gain, pb, wo, dy, dtab_words, dtab_scales,
                                      og, base, offs, offs2, out):
    nc = tc.nc
    add, mult, sub = ALU.add, ALU.mult, ALU.subtract

    with ExitStack() as ctx:
        lists = ctx.enter_context(tc.tile_pool(name="lists", bufs=1))
        keep = ctx.enter_context(tc.tile_pool(name="keep", bufs=1))
        psum = ctx.enter_context(tc.psum_pool(name="psum", bufs=1))

        def sb(name, width, dtype=F32, tag=None):
            return keep.tile([P, width], dtype, name=name, tag=tag or name, align_bytes=64)

        def grouped(ap):
            return ap.rearrange("p (g j) -> p g j", j=GS)

        def spread(ap):
            return ap.unsqueeze(2).to_broadcast([P, G, GS])

        offs_sb = lists.tile([P, J // 16], U16, name="offs_sb")
        offs2_sb = lists.tile([P, M // 16], U16, name="offs2_sb")

        tab_w, dtab_w = sb("tab_w", T, U32), sb("dtab_w", T, U32)
        tab_s = sb("tab_s", T, U8)
        w1_raw, wo_raw, dy_raw = sb("w1_raw", PACK * R, tag="w1_slot"), sb("wo_raw", PACK * R), sb("dy_raw", PACK * M)
        gain_sb, og_sb, pb_col = sb("gain_sb", 1), sb("og_sb", 1), sb("pb_col", 2)
        base_sb = sb("base_sb", J)
        placed = sb("placed", J)
        ident = sb("ident", P)

        def load_words(tile, words):
            nc.sync.dma_start(out=tile[:].bitcast(I32), in_=words[0].rearrange("p n t -> p (n t)").bitcast(I32))

        def load_scales(queue, tile, scales, quads):
            for quad in quads:
                queue.dma_start(out=tile[32 * quad:32 * quad + 4, :].bitcast(I32),
                                in_=scales[0, 4 * quad:4 * quad + 4, :].bitcast(I32))

        def load_rows(tile, rows):
            nc.sync.dma_start(out=tile[:], in_=rows.rearrange("(p t) w -> p (t w)", t=PACK))

        warm = sb("warm", 1)
        nc.vector.memset(warm[:], 1.0)
        nc.vector.memset(tab_s[:].bitcast(I32), 0)
        nc.vector.memset(placed[:], 0.0)
        warm2 = sb("warm2", 1)
        nc.scalar.activation(warm2[:], warm[:], ACT.Sqrt)

        nc.sync.dma_start(offs_sb[:], offs)
        nc.sync.dma_start(out=pb_col[:], in_=pb.rearrange("o (p h) -> (o p) h", h=2))
        load_rows(w1_raw, w1)
        load_scales(nc.sync, tab_s, tab_scales, range(4))
        load_words(tab_w, tab_words)
        nc.sync.dma_start(out=gain_sb[:], in_=gain)
        nc.sync.dma_start(offs2_sb[:], offs2)
        load_rows(dy_raw, dy)
        load_rows(wo_raw, wo)
        load_words(dtab_w, dtab_words)
        nc.sync.dma_start(out=base_sb[:], in_=base)
        nc.sync.dma_start(out=og_sb[:], in_=og)
        make_identity(nc, ident[:])

        def interleave(name, raw, width):
            woven = sb(name + "_bf", PACK * width, BF16)
            nc.scalar.copy(out=woven[:].rearrange("p (c i t) -> p c t i", t=PACK, i=4),
                           in_=raw[:].rearrange("p (t c i) -> p c t i", t=PACK, i=4))
            return woven

        def quantise(name, woven, width):
            codes, scales = sb(name + "_c", width, U32), sb(name + "_s", width, U8)
            nc.vector.quantize_mx(out=codes[:].bitcast(FP8X4), scales=scales[:], in_=woven[:])
            return codes, scales

        def gather_tab(name, window, dtype):
            picked = sb(name, J, dtype)
            nc.vector.tensor_copy(picked[:], window[:].indirect(offs_sb[:]))
            return picked

        def product(name, lhs, rhs, width):
            acc = psum.tile([P, width], F32, name=name)
            nc.tensor.matmul_mx(out=acc[:], lhsT=lhs[0][:].bitcast(FP8X4), lhsT_scale=lhs[1][:],
                                rhs=rhs[0][:].bitcast(FP8X4), rhs_scale=rhs[1][:], start=True, stop=True)
            return acc

        def tt(name, a, b, op):
            res = sb(name, M)
            nc.vector.tensor_tensor(res[:], a, b, op)
            return res

        def stt(name, a, scalar, b, op0, op1, width=M):
            res = sb(name, width)
            nc.vector.scalar_tensor_tensor(res[:], a, scalar, b, op0, op1)
            return res

        def stt_spread(name, small, scalar, b, op0, op1):
            res = sb(name, M)
            nc.vector.scalar_tensor_tensor(grouped(res[:]), spread(small), scalar, grouped(b), op0, op1)
            return res

        def act(name, a, func, width=M, **kw):
            res = sb(name, width)
            nc.scalar.activation(res[:], a, func, **kw)
            return res

        def group_sums(name, a, count=1):
            res = sb(name, count * G)
            nc.vector.tensor_reduce(res[:], grouped(a), AX.X, add)
            return res

        w1_bf = interleave("w1", w1_raw, R)
        pb_ps = psum.tile([P, 2, P], F32, name="pb_ps")
        for h in range(2):
            nc.tensor.transpose(pb_ps[:, h, :], pb_col[:, h:h + 1].to_broadcast([P, P]), ident[:])
        pb_full = sb("pb_full", M)
        nc.scalar.copy(out=pb_full[:].rearrange("p (n h) -> p n h", h=2), in_=pb_ps[:].rearrange("p h n -> p n h"))
        dtab_s = sb("dtab_s", T, U8, tag="w1_slot")
        nc.vector.memset(dtab_s[:].bitcast(I32), 0)
        load_scales(nc.scalar, dtab_s, dtab_scales, range(4))

        tab_gs = gather_tab("tab_gs", tab_s, U8)
        w1_q = quantise("w1", w1_bf, R)
        tab_gw = gather_tab("tab_gw", tab_w, U32)
        a_ps = product("a_ps", w1_q, (tab_gw, tab_gs), J)
        h1 = act("h1", a_ps[:], ACT.Copy, width=J, scale=gain_sb[:])
        dtab_gs = gather_tab("dtab_gs", dtab_s, U8)
        dy_bf = interleave("dy", dy_raw, M)
        wo_bf = interleave("wo", wo_raw, R)

        s = sb("s", M)
        nc.vector.tensor_tensor(s[:], h1[:].indirect(offs2_sb[:]), pb_full[:], add)
        s_sq = tt("s_sq", s[:], s[:], mult)
        sq_sum = group_sums("sq_sum", s_sq[:])
        q = act("q", sq_sum[:], ACT.Sqrt, width=G, scale=1.0 / GS, bias=0.1)
        dy_q = quantise("dy", dy_bf, M)
        rq = sb("rq", G)
        nc.vector.reciprocal(rq[:], q[:])
        wo_q = quantise("wo", wo_bf, R)
        c_ps = product("c_ps", wo_q, dy_q, M)
        u = sb("u", M)
        nc.vector.tensor_tensor(grouped(u[:]), grouped(s[:]), spread(rq[:]), mult)
        dtab_gw = gather_tab("dtab_gw", dtab_w, U32)
        ta_ps = product("ta_ps", w1_q, (dtab_gw, dtab_gs), J)

        silu_neg = act("silu_neg", u[:], ACT.Silu, scale=-1.0)
        th = act("th", u[:], ACT.Tanh, scale=-0.5)
        rq2 = sb("rq2", M, tag="s")
        nc.scalar.activation(grouped(rq2[:]), spread(rq[:]), ACT.Square, scale=math.sqrt(0.5))
        xh1 = act("xh1", ta_ps[:], ACT.Copy, width=J, scale=gain_sb[:])
        row_scale = act("row_scale", og_sb[:], ACT.Copy, width=1, scale=gain_sb[:])

        bend = stt("bend", u[:], 0.5, silu_neg[:], mult, add)
        c_sig = stt("c_sig", th[:], -1.0, c_ps[:], add, mult)
        c_bell = stt("c_bell", th[:], 1.0, c_sig[:], add, mult)
        f = stt("f", silu_neg[:], -1.0, c_sig[:], add, mult)
        g = stt("g", bend[:], -1.0, c_bell[:], add, mult)
        prods = sb("prods", 2 * M)
        nc.vector.tensor_tensor(prods[:, 0:M], f[:], u[:], mult)
        gu = tt("gu", g[:], u[:], mult)
        x = sb("x", M)
        nc.vector.tensor_tensor(x[:], xh1[:].indirect(offs2_sb[:]), rq2[:], mult)
        e = tt("e", gu[:], f[:], add)
        xprods = sb("xprods", 2 * M)
        nc.vector.tensor_tensor(xprods[:, 0:M], x[:], u[:], mult)
        nc.vector.tensor_tensor(prods[:, M:2 * M], e[:], u[:], mult)
        nc.vector.tensor_tensor(xprods[:, M:2 * M], x[:], e[:], mult)
        ab = group_sums("ab", prods[:], 2)
        pq = group_sums("pq", xprods[:], 2)
        sum_a, sum_b, sum_p, sum_q = ab[:, 0:G], ab[:, G:2 * G], pq[:, 0:G], pq[:, G:2 * G]
        d = stt("d", sum_a, 2.0, sum_b, mult, add, width=G)
        k = stt_spread("k", sum_a, -1.0 / GS, g[:], mult, add)
        pd = stt("pd", sum_p, 1.0 / GS, d[:], mult, mult, width=G)
        pe = stt_spread("pe", sum_p, -1.0 / GS, e[:], mult, mult)
        z = sb("z", G)
        nc.vector.tensor_tensor(z[:], pd[:], sum_q, sub)
        xk = tt("xk", x[:], k[:], mult)
        uz = stt_spread("uz", z[:], 1.0 / GS, u[:], mult, mult)
        part = tt("part", xk[:], pe[:], add)
        nc.vector.tensor_tensor(placed[:].indirect(offs2_sb[:]), part[:], uz[:], add)

        res = sb("res", J)
        half = J // 2
        for i, queue in enumerate((nc.sync, nc.scalar)):
            cols = slice(i * half, (i + 1) * half)
            nc.vector.scalar_tensor_tensor(res[:, cols], placed[:, cols], row_scale[:], base_sb[:, cols], mult, add)
            queue.dma_start(out=out[:, cols], in_=res[:, cols])
